import numpy as np
import ml_dtypes


def mxq(x, axis, fmt="e4m3"):
    dtype, down = {"e4m3": (ml_dtypes.float8_e4m3fn, 7), "e5m2": (ml_dtypes.float8_e5m2, 14)}[fmt]
    v = np.moveaxis(np.asarray(x, np.float32).astype(ml_dtypes.bfloat16).astype(np.float64), axis, -1)
    blocks = v.reshape(v.shape[:-1] + (-1, 32))
    amax = np.abs(blocks).max(-1, keepdims=True)
    byte = np.maximum(np.where(amax > 0, np.frexp(amax)[1] - 1 + 127, 0) - down, 1)
    scale = np.exp2(byte - 127.0)
    codes = (blocks / scale).astype(np.float32).astype(dtype).astype(np.float64)
    return np.moveaxis((codes * scale).reshape(v.shape), -1, axis)


WIDE = False


def mx_kscale(k):
    if not WIDE:
        return np.ones(k)
    levels = np.array([10, -10, 5, -5, 0])
    if k % 512:
        return np.exp2(np.random.permutation(np.resize(levels, k // 32))).repeat(32)
    a = np.empty((k // 512, 16))
    for p in range(k // 512):
        a[p, :8] = np.random.permutation(np.resize(levels, 8))
        for g in range(8):
            far = levels[np.abs(levels - a[p, g]) >= 10]
            a[p, g + 8] = far[np.random.randint(len(far))]
    return np.exp2(a.ravel()).repeat(32)


def f64(x):
    return np.asarray(x).astype(np.float64)


def striped(idx):
    return np.tile(idx.reshape(-1, 16).T, (8, 1)).astype(np.uint16)


def unstriped(offs):
    return offs[:16].T.reshape(-1).astype(np.int64)


E2M1 = np.array([0.0, 0.5, 1.0, 1.5, 2.0, 3.0, 4.0, 6.0, -0.0, -0.5, -1.0, -1.5, -2.0, -3.0, -4.0, -6.0])


def pack_weight(w, fmt):
    k, n = w.shape
    w = f64(np.asarray(w, np.float32).astype(ml_dtypes.bfloat16)).reshape(k // 32, 32, n)
    amax = np.abs(w).max(1)
    if fmt == "e4m3":
        byte = np.frexp(amax)[1] - 1 + 127 - 7
    else:
        mant, ex = np.frexp(amax / 6.0)
        byte = np.where(mant > 0.5, ex, ex - 1) + 127
    byte = np.clip(np.where(amax > 0, byte, 1), 1, 254)
    scaled = (w * np.exp2(127.0 - byte)[:, None, :]).reshape(k, n).astype(np.float32)
    by_word = np.ascontiguousarray(scaled.reshape(k // 512, 128, 4, n).transpose(0, 1, 3, 2))
    if fmt == "e4m3":
        words = by_word.astype(ml_dtypes.float8_e4m3fn).view(np.uint8)
    else:
        c = by_word.astype(ml_dtypes.float4_e2m1fn).view(np.uint8) & 0xF
        words = (c[..., 0::2] | (c[..., 1::2] << 4)).reshape(k // 512, 128, 2 * n)
    return np.ascontiguousarray(words), np.ascontiguousarray(byte.astype(np.uint8).reshape(k // 512, 16, n))


def unpack_weight(words, scales, fmt):
    g, _, n = scales.shape
    words = np.ascontiguousarray(words).reshape(g, 128, n, -1)
    if fmt == "e4m3":
        vals = words.view(ml_dtypes.float8_e4m3fn).astype(np.float64)
    else:
        nib = np.empty((g, 128, n, 4), np.uint8)
        nib[..., 0::2] = words & 0xF
        nib[..., 1::2] = words >> 4
        vals = E2M1[nib]
    vals = vals * np.repeat(np.exp2(scales.astype(np.float64) - 127.0), 8, axis=1)[..., None]
    return vals.transpose(0, 1, 3, 2).reshape(g * 512, n)


def gelu(v):
    return 0.5 * v * (1.0 + np.tanh(np.sqrt(2.0 / np.pi) * (v + 0.044715 * v**3)))


K, T, S, H, T2, P = 1024, 2048, 512, 1024, 1024, 512


def setup_inputs():
    n = np.random.standard_normal
    s = mx_kscale(K)[:, None]
    u = mx_kscale(H)[:, None]
    d = {}
    d["tab_words"], d["tab_scales"] = pack_weight(n((K, T)) * s, "e4m3")
    d["offs"] = striped(np.random.permutation(T)[:S])
    d["w1"] = (4.0 * n((K, H)) / K ** 0.5 / s).astype(np.float32)
    d["w4_words"], d["w4_scales"] = pack_weight(n((K, H)) / K ** 0.5 / s * u.T, "e2m1")
    d["wgs"] = np.exp(0.3 * n((128, S))).astype(np.float32)
    d["page0"] = (n((H, T2)) * u).astype(np.float32)
    d["offs2"] = striped(np.random.permutation(T2)[:S])
    d["offs3"] = striped(np.random.permutation(T2)[:P])
    d["base"] = (n((H, P)) * u).astype(np.float32)
    d["gv"] = (1.5 * n(H) / H ** 0.5 / u[:, 0] ** 2).astype(np.float32)
    d["slot"] = (0.8 * n(T2)).astype(np.float32)
    return d


def reference(tab_words, tab_scales, offs, w1, w4_words, w4_scales, wgs, page0, offs2, offs3, base, gv, slot):
    v = unpack_weight(tab_words, tab_scales, "e4m3")[:, unstriped(offs)]
    a = mxq(f64(w1), 0, "e4m3").T @ v
    b = unpack_weight(w4_words, w4_scales, "e2m1").T @ v
    h = np.log(np.abs(a) + 1.0) * b
    page = f64(page0).copy()
    page[:, unstriped(offs2)] = np.tile(f64(wgs), (H // 128, 1)) * h
    x = np.maximum(page[:, unstriped(offs3)], f64(base)) * f64(gv)[:, None]
    e = mxq(page, 0, "e4m3").T @ mxq(x, 0, "e4m3")
    return 1.0 / (1.0 + np.exp(-(e + f64(slot)[:, None])))

@@ -1,0 +1,284 @@
+from contextlib import ExitStack
+
+import concourse.mybir as mybir
+
+K, T, S, H, T2, NP = 1024, 2048, 512, 1024, 1024, 512
+FLOPS = 2 * (2 * K * H * S + H * T2 * NP)
+
+F32 = mybir.dt.float32
+BF16 = mybir.dt.bfloat16
+I32 = mybir.dt.int32
+U32 = mybir.dt.uint32
+U16 = mybir.dt.uint16
+U8 = mybir.dt.uint8
+FP8X4 = mybir.dt.float8_e4m3fn_x4
+FP4X4 = mybir.dt.float4_e2m1fn_x4
+ACT = mybir.ActivationFunctionType
+ALU = mybir.AluOpType
+P = 128
+
+
+def tile_list_drench_failure_page_kernel(
+    tc, tab_words, tab_scales, offs, w1, w4_words, w4_scales, wgs, page0, offs2, offs3, base, gv, slot, out
+):
+    nc = tc.nc
+    with ExitStack() as ctx:
+        keep = ctx.enter_context(tc.tile_pool(name="keep", bufs=1))
+        ring = ctx.enter_context(tc.tile_pool(name="ring", bufs=2))
+        psum = ctx.enter_context(tc.psum_pool(name="psum", bufs=1))
+
+        def held(name, shape, dtype):
+            return keep.tile(shape, dtype, name=name, align_bytes=64)
+
+        def turn(name, shape, dtype, bufs=2):
+            return ring.tile(shape, dtype, name=name, bufs=bufs, align_bytes=64)
+
+        list1 = held("list1", [P, S // 16], U16)
+        list2 = held("list2", [P, S // 16], U16)
+        list3 = held("list3", [P, NP // 16], U16)
+        w4_raw = [held(f"w4_raw{g}", [P, 2, H], U8) for g in range(2)]
+        w4_codes = [held(f"w4_codes{g}", [P, 2, H], U8) for g in range(2)]
+        w4s_raw = held("w4s_raw", [P, 2, H], U8)
+        tabs = held("tabs", [P, 2 * T], U8)
+        tabw = [held(f"tabw{a}", [P, T], I32) for a in range(2)]
+        gain = held("gain", [P, 4, S], F32)
+        page = [held(f"page{s}", [P, T2], F32) for s in range(8)]
+        floor = [held(f"floor{g}", [P, 4, NP], F32) for g in range(2)]
+        gv_sb = held("gv_sb", [P, 2, 4], F32)
+        slot_sb = held("slot_sb", [P, 8], F32)
+
+        nc.vector.memset(tabs[:].bitcast(I32), 0)
+        nc.vector.memset(w4s_raw[:].rearrange("p a c -> p (a c)").bitcast(I32), 0)
+
+        def load_w4_scales(q):
+            nc.scalar.dma_start(
+                out=w4s_raw[32 * q : 32 * q + 4].bitcast(I32),
+                in_=w4_scales[:, 4 * q : 4 * q + 4, :].rearrange("a r c -> r a c").bitcast(I32),
+            )
+
+        def load_w4(g):
+            nc.sync.dma_start(
+                out=w4_raw[g][:].bitcast(I32),
+                in_=w4_words[:, :, H * g : H * (g + 1)].rearrange("a p c -> p a c").bitcast(I32),
+            )
+
+        def deal_w4(g):
+            nc.vector.tensor_copy(
+                out=w4_codes[g][:].bitcast(U16).rearrange("p a (t m) -> p a m t", t=4),
+                in_=w4_raw[g][:].bitcast(U16).rearrange("p a (m t) -> p a m t", t=4),
+            )
+
+        def load_w1(a, g):
+            raw = turn("w1_raw", [P, 4, 512], F32, bufs=4)
+            nc.sync.dma_start(
+                out=raw[:], in_=w1[512 * a : 512 * (a + 1), 512 * g : 512 * (g + 1)].rearrange("(p j) c -> p j c", j=4)
+            )
+            return raw
+
+        def load_page(s):
+            g, t = divmod(s, 4)
+            nc.sync.dma_start(
+                out=page[s][:], in_=page0[512 * g : 512 * (g + 1), :].rearrange("(p t) m -> t p m", t=4)[t]
+            )
+
+        def load_floor(g):
+            nc.sync.dma_start(
+                out=floor[g][:], in_=base[512 * g : 512 * (g + 1), :].rearrange("(p t) j -> p t j", t=4)
+            )
+
+        w1_codes = [[held(f"w1c{a}{g}", [P, 512], U32) for g in range(2)] for a in range(2)]
+        w1_scales = [[held(f"w1s{a}{g}", [P, 512], U8) for g in range(2)] for a in range(2)]
+
+        def quantise_w1(a, g, raw):
+            rounded = turn("w1_bf", [P, 2048], BF16)
+            for part in (slice(0, 64), slice(64, P)) if g == 1 else (slice(0, P),):
+                nc.scalar.copy(
+                    out=rounded[:].rearrange("p (t m j) -> p m j t", t=4, j=4)[:, part],
+                    in_=raw[:].rearrange("p j (m t) -> p m j t", t=4)[:, part],
+                )
+            nc.vector.quantize_mx(out=w1_codes[a][g][:].bitcast(FP8X4), scales=w1_scales[a][g][:], in_=rounded[:])
+
+        def deal_w4_scales(g):
+            nc.vector.tensor_copy(
+                out=w4_sc[g][:].rearrange("p a (t m) -> p a m t", t=4),
+                in_=w4s_raw[:, :, 512 * g : 512 * (g + 1)].rearrange("p a (m t) -> p a m t", t=4),
+            )
+
+        w4_sc = [held(f"w4_sc{g}", [P, 2, 512], U8) for g in range(2)]
+        nc.sync.dma_start(list1[:], offs)
+        nc.sync.dma_start(list2[:], offs2)
+        nc.sync.dma_start(list3[:], offs3)
+        nc.sync.dma_start(out=gv_sb[:], in_=gv.rearrange("(g p t) -> p g t", g=2, t=4))
+        load_w4(0)
+        load_w4(1)
+        raws = [load_w1(a, 0) for a in range(2)]
+        for q in range(4):
+            nc.scalar.dma_start(
+                out=tabs[32 * q : 32 * q + 4, :].rearrange("p (a c) -> p a c", a=2).bitcast(I32),
+                in_=tab_scales[:, 4 * q : 4 * q + 4, :].rearrange("a r c -> r a c").bitcast(I32),
+            )
+        load_w4_scales(0)
+        load_w4_scales(1)
+        for a in range(2):
+            nc.sync.dma_start(out=tabw[a][:], in_=tab_words[a].rearrange("p n t -> p (n t)").bitcast(I32))
+        load_w4_scales(2)
+        load_w4_scales(3)
+        load_page(0)
+        for q in range(4):
+            nc.sync.dma_start(out=gain[32 * q : 32 * (q + 1)], in_=wgs.rearrange("(q t) j -> q t j", t=4))
+        load_page(1)
+
+        deal_w4(0)
+        for a in range(2):
+            quantise_w1(a, 0, raws[a])
+        v_codes = [held(f"vc{a}", [P, S], U32) for a in range(2)]
+        v_scales = [held(f"vs{a}", [P, S], U8) for a in range(2)]
+        for a in range(2):
+            nc.vector.tensor_copy(v_scales[a][:], tabs[:, T * a : T * (a + 1)].indirect(list1[:]))
+        for a in range(2):
+            nc.vector.tensor_copy(v_codes[a][:], tabw[a][:].bitcast(U32).indirect(list1[:]))
+        deal_w4_scales(0)
+        deal_w4(1)
+        deal_w4_scales(1)
+
+        raws = [load_w1(a, 1) for a in range(2)]
+        load_floor(0)
+        for s in range(2, 8):
+            load_page(s)
+        load_floor(1)
+        with nc.allow_non_contiguous_dma(reason="one value a partition"):
+            nc.sync.dma_start(out=slot_sb[:], in_=slot.rearrange("(u p) -> p u", p=P))
+
+        page_codes = [held(f"pc{g}", [P, T2], U32) for g in range(2)]
+        page_scales = [held(f"ps{g}", [P, T2], U8) for g in range(2)]
+        x_codes = [held(f"xc{g}", [P, NP], U32) for g in range(2)]
+        x_scales = [held(f"xs{g}", [P, NP], U8) for g in range(2)]
+        scores = {}
+
+        def score_pass(u, g):
+            if g == 0:
+                tag = f"e{u}" if u < 5 else "readout"
+                scores[u] = psum.tile([P, NP], F32, name=tag, bufs=1 if u < 5 else 3)
+            cols = slice(P * u, P * (u + 1))
+            nc.tensor.matmul_mx(
+                out=scores[u][:],
+                lhsT=page_codes[g][:, cols].bitcast(FP8X4),
+                lhsT_scale=page_scales[g][:, cols],
+                rhs=x_codes[g][:].bitcast(FP8X4),
+                rhs_scale=x_scales[g][:],
+                start=(g == 0),
+                stop=(g == 1),
+            )
+
+        page_pairs = [turn("page_pairs", [P, 2, T2, 2], BF16) for g in range(2)]
+        x_pairs = [turn("x_pairs", [P, 2, NP, 2], BF16) for g in range(2)]
+        logged = {}
+        gained = {}
+
+        def read_out(s):
+            g, t = divmod(s, 4)
+            a_ps = psum.tile([P, S], F32, name="readout", bufs=3)
+            b_ps = psum.tile([P, S], F32, name="readout", bufs=3)
+            for a in range(2):
+                nc.tensor.matmul_mx(
+                    out=a_ps[:],
+                    lhsT=w1_codes[a][g][:, P * t : P * (t + 1)].bitcast(FP8X4),
+                    lhsT_scale=w1_scales[a][g][:, P * t : P * (t + 1)],
+                    rhs=v_codes[a][:].bitcast(FP8X4),
+                    rhs_scale=v_scales[a][:],
+                    start=(a == 0),
+                    stop=(a == 1),
+                )
+            for a in range(2):
+                nc.tensor.matmul_mx(
+                    out=b_ps[:],
+                    lhsT=w4_codes[g][:, a, 2 * P * t : 2 * P * (t + 1)].bitcast(FP4X4),
+                    lhsT_scale=w4_sc[g][:, a, P * t : P * (t + 1)],
+                    rhs=v_codes[a][:].bitcast(FP8X4),
+                    rhs_scale=v_scales[a][:],
+                    start=(a == 0),
+                    stop=(a == 1),
+                )
+            size = turn("scratch", [P, S], F32, bufs=1)
+            nc.scalar.activation(out=size[:], in_=a_ps[:], func=ACT.Abs)
+            logged[s] = turn("logged", [P, S], F32)
+            nc.scalar.activation(out=logged[s][:], in_=size[:], func=ACT.Ln, bias=1.0)
+            if s == 7:
+                warm = held("warm", [P, 1], F32)
+                nc.scalar.activation(out=warm[:], in_=logged[s][:, 0:1], func=ACT.Sigmoid)
+            return b_ps
+
+        def apply_gain(s, b_ps):
+            gained[s] = turn("gained", [P, S], F32)
+            nc.vector.tensor_tensor(gained[s][:], b_ps[:], logged[s][:], ALU.mult)
+
+        def replace_columns(s):
+            nc.vector.tensor_tensor(page[s][:].indirect(list2[:]), gained[s][:], gain[:, s % 4, :], ALU.mult)
+
+        def round_page(s, halves):
+            g, t = divmod(s, 4)
+            for cols in halves:
+                nc.scalar.copy(out=page_pairs[g][:, t // 2, cols, t % 2], in_=page[s][:, cols])
+
+        def pick(s):
+            picked = turn("scratch", [P, NP], F32, bufs=1) if s < 6 else turn("picked", [P, NP], F32)
+            nc.vector.tensor_copy(picked[:], page[s][:].indirect(list3[:]))
+            return picked
+
+        def weigh(s, picked):
+            g, t = divmod(s, 4)
+            larger = turn("larger", [P, NP], F32)
+            nc.vector.tensor_tensor(larger[:], picked[:], floor[g][:, t, :], ALU.max)
+            return larger
+
+        def round_x(s, larger):
+            g, t = divmod(s, 4)
+            nc.scalar.activation(
+                out=x_pairs[g][:, t // 2, :, t % 2], in_=larger[:], func=ACT.Copy, scale=gv_sb[:, g, t : t + 1]
+            )
+
+        def weave(copy, pairs):
+            woven = turn("woven", [P, 2048], BF16, bufs=3)
+            copy(
+                out=woven[:].bitcast(F32).rearrange("p (c i u) -> p c u i", i=4, u=2),
+                in_=pairs.rearrange("p u c e -> p u (c e)").bitcast(F32).rearrange("p u (c i) -> p c u i", i=4),
+            )
+            return woven
+
+        def quantise(codes, scales, woven):
+            nc.vector.quantize_mx(out=codes.bitcast(FP8X4), scales=scales, in_=woven[:])
+
+        whole, halves = [slice(0, T2)], [slice(0, 512), slice(512, T2)]
+        b_ps = read_out(0)
+        for s in range(8):
+            picked = pick(s - 2) if s > 1 else None
+            apply_gain(s, b_ps)
+            larger = weigh(s - 2, picked) if s > 1 else None
+            if s < 7:
+                b_ps = read_out(s + 1)
+            if s > 1:
+                round_x(s - 2, larger)
+            if s == 7:
+                round_x(6, weigh(6, pick(6)))
+            replace_columns(s)
+            round_page(s, whole if s < 7 else halves)
+            if s in (0, 1):
+                quantise_w1(s, 1, raws[s])
+            if s == 3:
+                for cols in halves:
+                    quantise(page_codes[0][:, cols], page_scales[0][:, cols], weave(nc.scalar.copy, page_pairs[0][:, :, cols, :]))
+            if s == 5:
+                quantise(x_codes[0][:], x_scales[0][:], weave(nc.scalar.copy, x_pairs[0][:]))
+                for u in range(5):
+                    score_pass(u, 0)
+        for u in range(5, 8):
+            score_pass(u, 0)
+        round_x(7, weigh(7, pick(7)))
+        quantise(page_codes[1][:, halves[0]], page_scales[1][:, halves[0]], weave(nc.vector.tensor_copy, page_pairs[1][:, :, halves[0], :]))
+        quantise(x_codes[1][:], x_scales[1][:], weave(nc.vector.tensor_copy, x_pairs[1][:]))
+        quantise(page_codes[1][:, halves[1]], page_scales[1][:, halves[1]], weave(nc.scalar.copy, page_pairs[1][:, :, halves[1], :]))
+        for u in range(8):
+            score_pass(u, 1)
+            result = turn("result", [P, NP], F32, bufs=8)
+            nc.scalar.activation(out=result[:], in_=scores[u][:], func=ACT.Sigmoid, bias=slot_sb[:, u : u + 1])
+            nc.sync.dma_start(out=out[P * u : P * (u + 1), :], in_=result[:])

@@ -41,19 +41,23 @@ def tile_list_drench_failure_page_kernel(
         w4s_raw = held("w4s_raw", [P, 2, H], U8)
         tabs = held("tabs", [P, 2 * T], U8)
         tabw = [held(f"tabw{a}", [P, T], I32) for a in range(2)]
-        gain = held("gain", [P, 4, S], F32)
+        gain = [held(f"gain{u}", [P, 2, S], F32) for u in range(2)]
         page = [held(f"page{s}", [P, T2], F32) for s in range(8)]
-        floor = [held(f"floor{g}", [P, 4, NP], F32) for g in range(2)]
+        floor = [held(f"floor{n}", [P, 2, NP], F32) for n in range(4)]
         gv_sb = held("gv_sb", [P, 2, 4], F32)
         slot_sb = held("slot_sb", [P, 8], F32)
 
+        one = held("one", [P, 1], F32)
+        nc.gpsimd.memset(one[:], 1.0)
+        warm_ln = held("warm_ln", [P, 1], F32)
+        nc.scalar.activation(out=warm_ln[:], in_=one[:], func=ACT.Ln)
         nc.vector.memset(tabs[:].bitcast(I32), 0)
         nc.vector.memset(w4s_raw[:].rearrange("p a c -> p (a c)").bitcast(I32), 0)
 
         def load_w4_scales(q):
-            nc.scalar.dma_start(
-                out=w4s_raw[32 * q : 32 * q + 4].bitcast(I32),
-                in_=w4_scales[:, 4 * q : 4 * q + 4, :].rearrange("a r c -> r a c").bitcast(I32),
+            nc.sync.dma_start(
+                out=w4s_raw[q:P:32].bitcast(I32),
+                in_=w4_scales[:, q:16:4, :].rearrange("a r c -> r a c").bitcast(I32),
             )
 
         def load_w4(g):
@@ -64,8 +68,8 @@ def tile_list_drench_failure_page_kernel(
 
         def deal_w4(g):
             nc.vector.tensor_copy(
-                out=w4_codes[g][:].bitcast(U16).rearrange("p a (t m) -> p a m t", t=4),
-                in_=w4_raw[g][:].bitcast(U16).rearrange("p a (m t) -> p a m t", t=4),
+                out=w4_codes[g][:].bitcast(U16).rearrange("p a (t m) -> p a t m", t=4),
+                in_=w4_raw[g][:].bitcast(U16).rearrange("p a (m t) -> p a t m", t=4),
             )
 
         def load_w1(a, g):
@@ -75,16 +79,23 @@ def tile_list_drench_failure_page_kernel(
             )
             return raw
 
+        def load_gain(u):
+            for q in (0, 2, 1, 3):
+                nc.sync.dma_start(
+                    out=gain[u][32 * q : 32 * (q + 1)],
+                    in_=wgs.rearrange("(q t) j -> q t j", t=4)[:, 2 * u : 2 * u + 2, :],
+                )
+
         def load_page(s):
             g, t = divmod(s, 4)
             nc.sync.dma_start(
                 out=page[s][:], in_=page0[512 * g : 512 * (g + 1), :].rearrange("(p t) m -> t p m", t=4)[t]
             )
 
-        def load_floor(g):
-            nc.sync.dma_start(
-                out=floor[g][:], in_=base[512 * g : 512 * (g + 1), :].rearrange("(p t) j -> p t j", t=4)
-            )
+        def load_floor(n):
+            g, u = divmod(n, 2)
+            rows = base[512 * g : 512 * (g + 1), :].rearrange("(p t) j -> p t j", t=4)
+            nc.sync.dma_start(out=floor[n][:], in_=rows[:, 2 * u : 2 * u + 2, :])
 
         w1_codes = [[held(f"w1c{a}{g}", [P, 512], U32) for g in range(2)] for a in range(2)]
         w1_scales = [[held(f"w1s{a}{g}", [P, 512], U8) for g in range(2)] for a in range(2)]
@@ -100,8 +111,8 @@ def tile_list_drench_failure_page_kernel(
 
         def deal_w4_scales(g):
             nc.vector.tensor_copy(
-                out=w4_sc[g][:].rearrange("p a (t m) -> p a m t", t=4),
-                in_=w4s_raw[:, :, 512 * g : 512 * (g + 1)].rearrange("p a (m t) -> p a m t", t=4),
+                out=w4_sc[g][:].rearrange("p a (t m) -> p a t m", t=4),
+                in_=w4s_raw[:, :, 512 * g : 512 * (g + 1)].rearrange("p a (m t) -> p a t m", t=4),
             )
 
         w4_sc = [held(f"w4_sc{g}", [P, 2, 512], U8) for g in range(2)]
@@ -110,22 +121,19 @@ def tile_list_drench_failure_page_kernel(
         nc.sync.dma_start(list3[:], offs3)
         nc.sync.dma_start(out=gv_sb[:], in_=gv.rearrange("(g p t) -> p g t", g=2, t=4))
         load_w4(0)
-        load_w4(1)
         raws = [load_w1(a, 0) for a in range(2)]
         for q in range(4):
             nc.scalar.dma_start(
-                out=tabs[32 * q : 32 * q + 4, :].rearrange("p (a c) -> p a c", a=2).bitcast(I32),
-                in_=tab_scales[:, 4 * q : 4 * q + 4, :].rearrange("a r c -> r a c").bitcast(I32),
+                out=tabs[q:P:32, :].rearrange("p (a c) -> p a c", a=2).bitcast(I32),
+                in_=tab_scales[:, q:16:4, :].rearrange("a r c -> r a c").bitcast(I32),
             )
-        load_w4_scales(0)
-        load_w4_scales(1)
         for a in range(2):
             nc.sync.dma_start(out=tabw[a][:], in_=tab_words[a].rearrange("p n t -> p (n t)").bitcast(I32))
-        load_w4_scales(2)
-        load_w4_scales(3)
-        load_page(0)
         for q in range(4):
-            nc.sync.dma_start(out=gain[32 * q : 32 * (q + 1)], in_=wgs.rearrange("(q t) j -> q t j", t=4))
+            load_w4_scales(q)
+        load_w4(1)
+        load_page(0)
+        load_gain(0)
         load_page(1)
 
         deal_w4(0)
@@ -143,9 +151,14 @@ def tile_list_drench_failure_page_kernel(
 
         raws = [load_w1(a, 1) for a in range(2)]
         load_floor(0)
-        for s in range(2, 8):
-            load_page(s)
-        load_floor(1)
+        load_gain(1)
+        load_page(2)
+        load_page(3)
+        for n in range(1, 4):
+            load_floor(n)
+            if n < 3:
+                load_page(2 * n + 2)
+                load_page(2 * n + 3)
         with nc.allow_non_contiguous_dma(reason="one value a partition"):
             nc.sync.dma_start(out=slot_sb[:], in_=slot.rearrange("(u p) -> p u", p=P))
 
@@ -173,6 +186,8 @@ def tile_list_drench_failure_page_kernel(
         page_pairs = [turn("page_pairs", [P, 2, T2, 2], BF16) for g in range(2)]
         x_pairs = [turn("x_pairs", [P, 2, NP, 2], BF16) for g in range(2)]
         logged = {}
+        size = {}
+        second = {}
         gained = {}
 
         def read_out(s):
@@ -199,21 +214,23 @@ def tile_list_drench_failure_page_kernel(
                     start=(a == 0),
                     stop=(a == 1),
                 )
-            size = turn("scratch", [P, S], F32, bufs=1)
-            nc.scalar.activation(out=size[:], in_=a_ps[:], func=ACT.Abs)
-            logged[s] = turn("logged", [P, S], F32)
-            nc.scalar.activation(out=logged[s][:], in_=size[:], func=ACT.Ln, bias=1.0)
+            size[s] = turn(f"scratch{s % 2}", [P, S], F32, bufs=1)
+            nc.scalar.activation(out=size[s][:], in_=a_ps[:], func=ACT.Abs)
+            second[s] = b_ps
+
+        def take_log(s):
+            logged[s] = turn("logged", [P, S], F32, bufs=1)
+            nc.scalar.activation(out=logged[s][:], in_=size[s][:], func=ACT.Ln, bias=1.0)
             if s == 7:
                 warm = held("warm", [P, 1], F32)
                 nc.scalar.activation(out=warm[:], in_=logged[s][:, 0:1], func=ACT.Sigmoid)
-            return b_ps
 
-        def apply_gain(s, b_ps):
+        def apply_gain(s):
             gained[s] = turn("gained", [P, S], F32)
-            nc.vector.tensor_tensor(gained[s][:], b_ps[:], logged[s][:], ALU.mult)
+            nc.vector.tensor_tensor(gained[s][:], second[s][:], logged[s][:], ALU.mult)
 
         def replace_columns(s):
-            nc.vector.tensor_tensor(page[s][:].indirect(list2[:]), gained[s][:], gain[:, s % 4, :], ALU.mult)
+            nc.vector.tensor_tensor(page[s][:].indirect(list2[:]), gained[s][:], gain[s % 4 // 2][:, s % 2, :], ALU.mult)
 
         def round_page(s, halves):
             g, t = divmod(s, 4)
@@ -221,14 +238,13 @@ def tile_list_drench_failure_page_kernel(
                 nc.scalar.copy(out=page_pairs[g][:, t // 2, cols, t % 2], in_=page[s][:, cols])
 
         def pick(s):
-            picked = turn("scratch", [P, NP], F32, bufs=1) if s < 6 else turn("picked", [P, NP], F32)
+            picked = turn(f"scratch{s % 2}", [P, NP], F32, bufs=1) if s < 6 else turn("picked", [P, NP], F32)
             nc.vector.tensor_copy(picked[:], page[s][:].indirect(list3[:]))
             return picked
 
         def weigh(s, picked):
-            g, t = divmod(s, 4)
             larger = turn("larger", [P, NP], F32)
-            nc.vector.tensor_tensor(larger[:], picked[:], floor[g][:, t, :], ALU.max)
+            nc.vector.tensor_tensor(larger[:], picked[:], floor[s // 2][:, s % 2, :], ALU.max)
             return larger
 
         def round_x(s, larger):
@@ -238,7 +254,7 @@ def tile_list_drench_failure_page_kernel(
             )
 
         def weave(copy, pairs):
-            woven = turn("woven", [P, 2048], BF16, bufs=3)
+            woven = turn("woven", [P, 2048], BF16)
             copy(
                 out=woven[:].bitcast(F32).rearrange("p (c i u) -> p c u i", i=4, u=2),
                 in_=pairs.rearrange("p u c e -> p u (c e)").bitcast(F32).rearrange("p u (c i) -> p c u i", i=4),
@@ -249,13 +265,17 @@ def tile_list_drench_failure_page_kernel(
             nc.vector.quantize_mx(out=codes.bitcast(FP8X4), scales=scales, in_=woven[:])
 
         whole, halves = [slice(0, T2)], [slice(0, 512), slice(512, T2)]
-        b_ps = read_out(0)
+        read_out(0)
+        take_log(0)
+        read_out(1)
         for s in range(8):
             picked = pick(s - 2) if s > 1 else None
-            apply_gain(s, b_ps)
+            apply_gain(s)
             larger = weigh(s - 2, picked) if s > 1 else None
             if s < 7:
-                b_ps = read_out(s + 1)
+                take_log(s + 1)
+            if s < 6:
+                read_out(s + 2)
             if s > 1:
                 round_x(s - 2, larger)
             if s == 7:

from contextlib import ExitStack

import concourse.mybir as mybir

K, T, S, H, T2, NP = 1024, 2048, 512, 1024, 1024, 512
FLOPS = 2 * (2 * K * H * S + H * T2 * NP)

F32 = mybir.dt.float32
BF16 = mybir.dt.bfloat16
I32 = mybir.dt.int32
U32 = mybir.dt.uint32
U16 = mybir.dt.uint16
U8 = mybir.dt.uint8
FP8X4 = mybir.dt.float8_e4m3fn_x4
FP4X4 = mybir.dt.float4_e2m1fn_x4
ACT = mybir.ActivationFunctionType
ALU = mybir.AluOpType
P = 128


def tile_list_drench_failure_page_kernel(
    tc, tab_words, tab_scales, offs, w1, w4_words, w4_scales, wgs, page0, offs2, offs3, base, gv, slot, out
):
    nc = tc.nc
    with ExitStack() as ctx:
        keep = ctx.enter_context(tc.tile_pool(name="keep", bufs=1))
        ring = ctx.enter_context(tc.tile_pool(name="ring", bufs=2))
        psum = ctx.enter_context(tc.psum_pool(name="psum", bufs=1))

        def held(name, shape, dtype):
            return keep.tile(shape, dtype, name=name, align_bytes=64)

        def turn(name, shape, dtype, bufs=2):
            return ring.tile(shape, dtype, name=name, bufs=bufs, align_bytes=64)

        list1 = held("list1", [P, S // 16], U16)
        list2 = held("list2", [P, S // 16], U16)
        list3 = held("list3", [P, NP // 16], U16)
        w4_raw = [held(f"w4_raw{g}", [P, 2, H], U8) for g in range(2)]
        w4_codes = [held(f"w4_codes{g}", [P, 2, H], U8) for g in range(2)]
        w4s_raw = held("w4s_raw", [P, 2, H], U8)
        tabs = held("tabs", [P, 2 * T], U8)
        tabw = [held(f"tabw{a}", [P, T], I32) for a in range(2)]
        gain = [held(f"gain{u}", [P, 2, S], F32) for u in range(2)]
        page = [held(f"page{s}", [P, T2], F32) for s in range(8)]
        floor = [held(f"floor{n}", [P, 2, NP], F32) for n in range(4)]
        gv_sb = held("gv_sb", [P, 2, 4], F32)
        slot_sb = held("slot_sb", [P, 8], F32)

        one = held("one", [P, 1], F32)
        nc.gpsimd.memset(one[:], 1.0)
        warm_ln = held("warm_ln", [P, 1], F32)
        nc.scalar.activation(out=warm_ln[:], in_=one[:], func=ACT.Ln)
        nc.vector.memset(tabs[:].bitcast(I32), 0)
        nc.vector.memset(w4s_raw[:].rearrange("p a c -> p (a c)").bitcast(I32), 0)

        def load_w4_scales(q):
            nc.sync.dma_start(
                out=w4s_raw[q:P:32].bitcast(I32),
                in_=w4_scales[:, q:16:4, :].rearrange("a r c -> r a c").bitcast(I32),
            )

        def load_w4(g):
            nc.sync.dma_start(
                out=w4_raw[g][:].bitcast(I32),
                in_=w4_words[:, :, H * g : H * (g + 1)].rearrange("a p c -> p a c").bitcast(I32),
            )

        def deal_w4(g):
            nc.vector.tensor_copy(
                out=w4_codes[g][:].bitcast(U16).rearrange("p a (t m) -> p a t m", t=4),
                in_=w4_raw[g][:].bitcast(U16).rearrange("p a (m t) -> p a t m", t=4),
            )

        def load_w1(a, g):
            raw = turn("w1_raw", [P, 4, 512], F32, bufs=4)
            nc.sync.dma_start(
                out=raw[:], in_=w1[512 * a : 512 * (a + 1), 512 * g : 512 * (g + 1)].rearrange("(p j) c -> p j c", j=4)
            )
            return raw

        def load_gain(u):
            for q in (0, 2, 1, 3):
                nc.sync.dma_start(
                    out=gain[u][32 * q : 32 * (q + 1)],
                    in_=wgs.rearrange("(q t) j -> q t j", t=4)[:, 2 * u : 2 * u + 2, :],
                )

        def load_page(s):
            g, t = divmod(s, 4)
            nc.sync.dma_start(
                out=page[s][:], in_=page0[512 * g : 512 * (g + 1), :].rearrange("(p t) m -> t p m", t=4)[t]
            )

        def load_floor(n):
            g, u = divmod(n, 2)
            rows = base[512 * g : 512 * (g + 1), :].rearrange("(p t) j -> p t j", t=4)
            nc.sync.dma_start(out=floor[n][:], in_=rows[:, 2 * u : 2 * u + 2, :])

        w1_codes = [[held(f"w1c{a}{g}", [P, 512], U32) for g in range(2)] for a in range(2)]
        w1_scales = [[held(f"w1s{a}{g}", [P, 512], U8) for g in range(2)] for a in range(2)]

        def quantise_w1(a, g, raw):
            rounded = turn("w1_bf", [P, 2048], BF16)
            for part in (slice(0, 64), slice(64, P)) if g == 1 else (slice(0, P),):
                nc.scalar.copy(
                    out=rounded[:].rearrange("p (t m j) -> p m j t", t=4, j=4)[:, part],
                    in_=raw[:].rearrange("p j (m t) -> p m j t", t=4)[:, part],
                )
            nc.vector.quantize_mx(out=w1_codes[a][g][:].bitcast(FP8X4), scales=w1_scales[a][g][:], in_=rounded[:])

        def deal_w4_scales(g):
            nc.vector.tensor_copy(
                out=w4_sc[g][:].rearrange("p a (t m) -> p a t m", t=4),
                in_=w4s_raw[:, :, 512 * g : 512 * (g + 1)].rearrange("p a (m t) -> p a t m", t=4),
            )

        w4_sc = [held(f"w4_sc{g}", [P, 2, 512], U8) for g in range(2)]
        nc.sync.dma_start(list1[:], offs)
        nc.sync.dma_start(list2[:], offs2)
        nc.sync.dma_start(list3[:], offs3)
        nc.sync.dma_start(out=gv_sb[:], in_=gv.rearrange("(g p t) -> p g t", g=2, t=4))
        load_w4(0)
        raws = [load_w1(a, 0) for a in range(2)]
        for q in range(4):
            nc.scalar.dma_start(
                out=tabs[q:P:32, :].rearrange("p (a c) -> p a c", a=2).bitcast(I32),
                in_=tab_scales[:, q:16:4, :].rearrange("a r c -> r a c").bitcast(I32),
            )
        for a in range(2):
            nc.sync.dma_start(out=tabw[a][:], in_=tab_words[a].rearrange("p n t -> p (n t)").bitcast(I32))
        for q in range(4):
            load_w4_scales(q)
        load_w4(1)
        load_page(0)
        load_gain(0)
        load_page(1)

        deal_w4(0)
        for a in range(2):
            quantise_w1(a, 0, raws[a])
        v_codes = [held(f"vc{a}", [P, S], U32) for a in range(2)]
        v_scales = [held(f"vs{a}", [P, S], U8) for a in range(2)]
        for a in range(2):
            nc.vector.tensor_copy(v_scales[a][:], tabs[:, T * a : T * (a + 1)].indirect(list1[:]))
        for a in range(2):
            nc.vector.tensor_copy(v_codes[a][:], tabw[a][:].bitcast(U32).indirect(list1[:]))
        deal_w4_scales(0)
        deal_w4(1)
        deal_w4_scales(1)

        raws = [load_w1(a, 1) for a in range(2)]
        load_floor(0)
        load_gain(1)
        load_page(2)
        load_page(3)
        for n in range(1, 4):
            load_floor(n)
            if n < 3:
                load_page(2 * n + 2)
                load_page(2 * n + 3)
        with nc.allow_non_contiguous_dma(reason="one value a partition"):
            nc.sync.dma_start(out=slot_sb[:], in_=slot.rearrange("(u p) -> p u", p=P))

        page_codes = [held(f"pc{g}", [P, T2], U32) for g in range(2)]
        page_scales = [held(f"ps{g}", [P, T2], U8) for g in range(2)]
        x_codes = [held(f"xc{g}", [P, NP], U32) for g in range(2)]
        x_scales = [held(f"xs{g}", [P, NP], U8) for g in range(2)]
        scores = {}

        def score_pass(u, g):
            if g == 0:
                tag = f"e{u}" if u < 5 else "readout"
                scores[u] = psum.tile([P, NP], F32, name=tag, bufs=1 if u < 5 else 3)
            cols = slice(P * u, P * (u + 1))
            nc.tensor.matmul_mx(
                out=scores[u][:],
                lhsT=page_codes[g][:, cols].bitcast(FP8X4),
                lhsT_scale=page_scales[g][:, cols],
                rhs=x_codes[g][:].bitcast(FP8X4),
                rhs_scale=x_scales[g][:],
                start=(g == 0),
                stop=(g == 1),
            )

        page_pairs = [turn("page_pairs", [P, 2, T2, 2], BF16) for g in range(2)]
        x_pairs = [turn("x_pairs", [P, 2, NP, 2], BF16) for g in range(2)]
        logged = {}
        size = {}
        second = {}
        gained = {}

        def read_out(s):
            g, t = divmod(s, 4)
            a_ps = psum.tile([P, S], F32, name="readout", bufs=3)
            b_ps = psum.tile([P, S], F32, name="readout", bufs=3)
            for a in range(2):
                nc.tensor.matmul_mx(
                    out=a_ps[:],
                    lhsT=w1_codes[a][g][:, P * t : P * (t + 1)].bitcast(FP8X4),
                    lhsT_scale=w1_scales[a][g][:, P * t : P * (t + 1)],
                    rhs=v_codes[a][:].bitcast(FP8X4),
                    rhs_scale=v_scales[a][:],
                    start=(a == 0),
                    stop=(a == 1),
                )
            for a in range(2):
                nc.tensor.matmul_mx(
                    out=b_ps[:],
                    lhsT=w4_codes[g][:, a, 2 * P * t : 2 * P * (t + 1)].bitcast(FP4X4),
                    lhsT_scale=w4_sc[g][:, a, P * t : P * (t + 1)],
                    rhs=v_codes[a][:].bitcast(FP8X4),
                    rhs_scale=v_scales[a][:],
                    start=(a == 0),
                    stop=(a == 1),
                )
            size[s] = turn(f"scratch{s % 2}", [P, S], F32, bufs=1)
            nc.scalar.activation(out=size[s][:], in_=a_ps[:], func=ACT.Abs)
            second[s] = b_ps

        def take_log(s):
            logged[s] = turn("logged", [P, S], F32, bufs=1)
            nc.scalar.activation(out=logged[s][:], in_=size[s][:], func=ACT.Ln, bias=1.0)
            if s == 7:
                warm = held("warm", [P, 1], F32)
                nc.scalar.activation(out=warm[:], in_=logged[s][:, 0:1], func=ACT.Sigmoid)

        def apply_gain(s):
            gained[s] = turn("gained", [P, S], F32)
            nc.vector.tensor_tensor(gained[s][:], second[s][:], logged[s][:], ALU.mult)

        def replace_columns(s):
            nc.vector.tensor_tensor(page[s][:].indirect(list2[:]), gained[s][:], gain[s % 4 // 2][:, s % 2, :], ALU.mult)

        def round_page(s, halves):
            g, t = divmod(s, 4)
            for cols in halves:
                nc.scalar.copy(out=page_pairs[g][:, t // 2, cols, t % 2], in_=page[s][:, cols])

        def pick(s):
            picked = turn(f"scratch{s % 2}", [P, NP], F32, bufs=1) if s < 6 else turn("picked", [P, NP], F32)
            nc.vector.tensor_copy(picked[:], page[s][:].indirect(list3[:]))
            return picked

        def weigh(s, picked):
            larger = turn("larger", [P, NP], F32)
            nc.vector.tensor_tensor(larger[:], picked[:], floor[s // 2][:, s % 2, :], ALU.max)
            return larger

        def round_x(s, larger):
            g, t = divmod(s, 4)
            nc.scalar.activation(
                out=x_pairs[g][:, t // 2, :, t % 2], in_=larger[:], func=ACT.Copy, scale=gv_sb[:, g, t : t + 1]
            )

        def weave(copy, pairs):
            woven = turn("woven", [P, 2048], BF16)
            copy(
                out=woven[:].bitcast(F32).rearrange("p (c i u) -> p c u i", i=4, u=2),
                in_=pairs.rearrange("p u c e -> p u (c e)").bitcast(F32).rearrange("p u (c i) -> p c u i", i=4),
            )
            return woven

        def quantise(codes, scales, woven):
            nc.vector.quantize_mx(out=codes.bitcast(FP8X4), scales=scales, in_=woven[:])

        whole, halves = [slice(0, T2)], [slice(0, 512), slice(512, T2)]
        read_out(0)
        take_log(0)
        read_out(1)
        for s in range(8):
            picked = pick(s - 2) if s > 1 else None
            apply_gain(s)
            larger = weigh(s - 2, picked) if s > 1 else None
            if s < 7:
                take_log(s + 1)
            if s < 6:
                read_out(s + 2)
            if s > 1:
                round_x(s - 2, larger)
            if s == 7:
                round_x(6, weigh(6, pick(6)))
            replace_columns(s)
            round_page(s, whole if s < 7 else halves)
            if s in (0, 1):
                quantise_w1(s, 1, raws[s])
            if s == 3:
                for cols in halves:
                    quantise(page_codes[0][:, cols], page_scales[0][:, cols], weave(nc.scalar.copy, page_pairs[0][:, :, cols, :]))
            if s == 5:
                quantise(x_codes[0][:], x_scales[0][:], weave(nc.scalar.copy, x_pairs[0][:]))
                for u in range(5):
                    score_pass(u, 0)
        for u in range(5, 8):
            score_pass(u, 0)
        round_x(7, weigh(7, pick(7)))
        quantise(page_codes[1][:, halves[0]], page_scales[1][:, halves[0]], weave(nc.vector.tensor_copy, page_pairs[1][:, :, halves[0], :]))
        quantise(x_codes[1][:], x_scales[1][:], weave(nc.vector.tensor_copy, x_pairs[1][:]))
        quantise(page_codes[1][:, halves[1]], page_scales[1][:, halves[1]], weave(nc.scalar.copy, page_pairs[1][:, :, halves[1], :]))
        for u in range(8):
            score_pass(u, 1)
            result = turn("result", [P, NP], F32, bufs=8)
            nc.scalar.activation(out=result[:], in_=scores[u][:], func=ACT.Sigmoid, bias=slot_sb[:, u : u + 1])
            nc.sync.dma_start(out=out[P * u : P * (u + 1), :], in_=result[:])
